import numpy as np
import ml_dtypes


def mxq(x, axis, fmt="e4m3"):
    dtype, down = {"e4m3": (ml_dtypes.float8_e4m3fn, 7), "e5m2": (ml_dtypes.float8_e5m2, 14)}[fmt]
    v = np.moveaxis(np.asarray(x, np.float32).astype(ml_dtypes.bfloat16).astype(np.float64), axis, -1)
    blocks = v.reshape(v.shape[:-1] + (-1, 32))
    amax = np.abs(blocks).max(-1, keepdims=True)
    byte = np.maximum(np.where(amax > 0, np.frexp(amax)[1] - 1 + 127, 0) - down, 1)
    scale = np.exp2(byte - 127.0)
    codes = (blocks / scale).astype(np.float32).astype(dtype).astype(np.float64)
    return np.moveaxis((codes * scale).reshape(v.shape), -1, axis)


WIDE = False


def mx_kscale(k):
    if not WIDE:
        return np.ones(k)
    levels = np.array([10, -10, 5, -5, 0])
    if k % 512:
        return np.exp2(np.random.permutation(np.resize(levels, k // 32))).repeat(32)
    a = np.empty((k // 512, 16))
    for p in range(k // 512):
        a[p, :8] = np.random.permutation(np.resize(levels, 8))
        for g in range(8):
            far = levels[np.abs(levels - a[p, g]) >= 10]
            a[p, g + 8] = far[np.random.randint(len(far))]
    return np.exp2(a.ravel()).repeat(32)


def f64(x):
    return np.asarray(x).astype(np.float64)


def striped(idx):
    return np.tile(np.asarray(idx).reshape(-1, 16).T, (8, 1)).astype(np.uint16)


def unstriped(offs):
    return offs[:16].T.reshape(-1).astype(np.int64)


E2M1 = np.array([0.0, 0.5, 1.0, 1.5, 2.0, 3.0, 4.0, 6.0, -0.0, -0.5, -1.0, -1.5, -2.0, -3.0, -4.0, -6.0])


def pack_weight(w, fmt):
    k, n = w.shape
    w = f64(np.asarray(w, np.float32).astype(ml_dtypes.bfloat16)).reshape(k // 32, 32, n)
    amax = np.abs(w).max(1)
    if fmt == "e4m3":
        byte = np.frexp(amax)[1] - 1 + 127 - 7
    else:
        mant, ex = np.frexp(amax / 6.0)
        byte = np.where(mant > 0.5, ex, ex - 1) + 127
    byte = np.clip(np.where(amax > 0, byte, 1), 1, 254)
    scaled = (w * np.exp2(127.0 - byte)[:, None, :]).reshape(k, n).astype(np.float32)
    by_word = np.ascontiguousarray(scaled.reshape(k // 512, 128, 4, n).transpose(0, 1, 3, 2))
    if fmt == "e4m3":
        words = by_word.astype(ml_dtypes.float8_e4m3fn).view(np.uint8)
    else:
        c = by_word.astype(ml_dtypes.float4_e2m1fn).view(np.uint8) & 0xF
        words = (c[..., 0::2] | (c[..., 1::2] << 4)).reshape(k // 512, 128, 2 * n)
    return np.ascontiguousarray(words), np.ascontiguousarray(byte.astype(np.uint8).reshape(k // 512, 16, n))


def unpack_weight(words, scales, fmt):
    g, _, n = scales.shape
    words = np.ascontiguousarray(words).reshape(g, 128, n, -1)
    if fmt == "e4m3":
        vals = words.view(ml_dtypes.float8_e4m3fn).astype(np.float64)
    else:
        nib = np.empty((g, 128, n, 4), np.uint8)
        nib[..., 0::2] = words & 0xF
        nib[..., 1::2] = words >> 4
        vals = E2M1[nib]
    vals = vals * np.repeat(np.exp2(scales.astype(np.float64) - 127.0), 8, axis=1)[..., None]
    return vals.transpose(0, 1, 3, 2).reshape(g * 512, n)


D, K, T, M, I, E = 512, 512, 2048, 1024, 512, 256


def setup_inputs():
    n = np.random.standard_normal
    idx = np.random.permutation(T)[:I]
    idx2 = np.random.permutation(M)[:I]
    idx3 = np.random.permutation(M)[:I]
    fd = mx_kscale(D)
    fk = mx_kscale(K)
    pagesp = pack_weight(n((D, T)) / fd[:, None], "e2m1")
    wap = pack_weight(n((D, K)) * 1.0 / np.sqrt(D) * fd[:, None], "e4m3")
    wop = pack_weight(n((K, E)) * 1.0 / np.sqrt(K) / fk[:, None], "e4m3")
    return {
        "pages_words": pagesp[0],
        "pages_scales": pagesp[1],
        "wa_words": wap[0],
        "wa_scales": wap[1],
        "kf": (np.random.uniform(0.5, 2.0, (K, 1)) * fk[:, None]).astype(np.float32),
        "wo_words": wop[0],
        "wo_scales": wop[1],
        "store": (1.0 * n((E, M))).astype(np.float32),
        "offs": striped(idx),
        "offs2": striped(idx2),
        "offs3": striped(idx3),
    }


def reference(pages_words, pages_scales, wa_words, wa_scales, kf, wo_words, wo_scales, store, offs, offs2, offs3):
    idx = unstriped(offs)
    idx2 = unstriped(offs2)
    idx3 = unstriped(offs3)
    pagesu = unpack_weight(pages_words, pages_scales, "e2m1")
    wau = unpack_weight(wa_words, wa_scales, "e4m3")
    wou = unpack_weight(wo_words, wo_scales, "e4m3")
    pagesidxg = pagesu[:, idx]
    z = wau.T @ pagesidxg
    w = z * f64(kf)
    wq = mxq(w, 0, "e4m3")
    o = wou.T @ wq
    f1 = np.zeros((E, M))
    f1[:, idx2] = o
    c1 = f64(store) + f1
    y = c1[:, idx3] - o
    return y

@@ -1,0 +1,217 @@
+from contextlib import ExitStack
+
+import concourse.mybir as mybir
+
+D, K, T, M, I, E = 512, 512, 2048, 1024, 512, 256
+FLOPS = 2 * D * K * I + 2 * K * E * I
+
+F32 = mybir.dt.float32
+BF16 = mybir.dt.bfloat16
+I32 = mybir.dt.int32
+U32 = mybir.dt.uint32
+U16 = mybir.dt.uint16
+U8 = mybir.dt.uint8
+FP8X4 = mybir.dt.float8_e4m3fn_x4
+FP4X4 = mybir.dt.float4_e2m1fn_x4
+MULT = mybir.AluOpType.mult
+ADD = mybir.AluOpType.add
+SUBTRACT = mybir.AluOpType.subtract
+COPY = mybir.ActivationFunctionType.Copy
+
+P = 128
+PACK = 4
+LIST_ROWS = 16
+HALF = 256
+QUARTER = 128
+BLOCKS = E // P
+
+
+def load_scale_rows(queue, plane, rows, q):
+    queue.dma_start(out=plane[32 * q : 32 * q + 4, :].bitcast(I32), in_=rows[4 * q : 4 * q + 4, :].bitcast(I32))
+
+
+def load_scale_rows_repeated(queue, plane, rows, q):
+    words = rows[4 * q : 4 * q + 4, :].bitcast(I32)
+    queue.dma_start(
+        out=plane[32 * q : 32 * q + 32, :].bitcast(I32),
+        in_=words.unsqueeze(0).to_broadcast([8, 4, words.shape[1]]),
+    )
+
+
+def entries(offsets, first, count):
+    return offsets[:, first // LIST_ROWS : (first + count) // LIST_ROWS]
+
+
+def tile_attend_outputsback_kernel(
+    tc, pages_words, pages_scales, wa_words, wa_scales, kf, wo_words, wo_scales, store, offs, offs2, offs3, out
+):
+    nc = tc.nc
+    with ExitStack() as ctx:
+        sb = ctx.enter_context(tc.tile_pool(name="sb", bufs=1))
+        psum = ctx.enter_context(tc.psum_pool(name="psum", bufs=1))
+
+        page_list = sb.tile([P, I // LIST_ROWS], U16, name="page_list")
+        put_list = sb.tile([P, I // LIST_ROWS], U16, name="put_list")
+        get_list = sb.tile([P, I // LIST_ROWS], U16, name="get_list")
+        page_words = sb.tile([P, T], U16, name="page_words", tag="early_late_1", align_bytes=64)
+        page_scales = sb.tile([P, T], U8, name="page_scales", align_bytes=64)
+        wa_raw = sb.tile([P, K], U32, name="wa_raw", tag="early_late_0", align_bytes=64)
+        wa_raw_scales = sb.tile([P, K], U8, name="wa_raw_scales", align_bytes=64)
+        wa_dealt = sb.tile([P, K], U32, name="wa_dealt", align_bytes=64)
+        wa_dealt_scales = sb.tile([P, K], U8, name="wa_dealt_scales", align_bytes=64)
+        wo_sb = sb.tile([P, E], U32, name="wo_sb", align_bytes=64)
+        wo_sb_scales = sb.tile([P, E], U8, name="wo_sb_scales", align_bytes=64)
+        kf_sb = sb.tile([P, PACK], F32, name="kf_sb")
+        placed = [sb.tile([P, M], F32, name=f"placed{b}") for b in range(BLOCKS)]
+
+        nc.vector.memset(wo_sb_scales[:].bitcast(I32), 0)
+        for b in range(BLOCKS):
+            nc.vector.memset(placed[b][:], 0.0)
+
+        nc.sync.dma_start(page_list[:], offs)
+        for q in range(2):
+            load_scale_rows_repeated(nc.sync, page_scales, pages_scales[0], q)
+        nc.sync.dma_start(out=page_words[:].bitcast(I32), in_=pages_words[0].bitcast(I32))
+        for q in range(2, 4):
+            load_scale_rows_repeated(nc.sync, page_scales, pages_scales[0], q)
+        load_scale_rows_repeated(nc.sync, wa_raw_scales, wa_scales[0], 0)
+        nc.sync.dma_start(out=wa_raw[:].bitcast(I32), in_=wa_words[0].rearrange("p n t -> p (n t)").bitcast(I32))
+        for q in range(1, 4):
+            load_scale_rows_repeated(nc.sync, wa_raw_scales, wa_scales[0], q)
+        nc.gpsimd.dma_start(out=kf_sb[:], in_=kf.rearrange("(p t) one -> p (t one)", t=PACK))
+        nc.gpsimd.dma_start(out=wo_sb[:].bitcast(I32), in_=wo_words[0].rearrange("p n t -> p (n t)").bitcast(I32))
+        for q in range(4):
+            load_scale_rows(nc.sync, wo_sb_scales, wo_scales[0], q)
+        nc.sync.dma_start(put_list[:], offs2)
+        nc.sync.dma_start(get_list[:], offs3)
+
+        nc.scalar.copy(
+            out=wa_dealt[:].rearrange("p (t m) -> p t m", t=PACK),
+            in_=wa_raw[:].rearrange("p (m t) -> p t m", t=PACK),
+        )
+        picked_words = [sb.tile([P, HALF], U16, name=f"picked_words{h}", align_bytes=64) for h in range(2)]
+        picked_scales = {}
+
+        def gather_words(h):
+            nc.vector.tensor_copy(picked_words[h][:], page_words[:].indirect(entries(page_list, h * HALF, HALF)))
+
+        def gather_scales(h):
+            picked = sb.tile([P, HALF], U8, name=f"picked_scales{h}", tag=f"after_quantise{h}", align_bytes=64)
+            nc.vector.tensor_copy(picked[:], page_scales[:].indirect(entries(page_list, h * HALF, HALF)))
+            picked_scales.setdefault(h, picked)
+
+        gather_words(0)
+        gather_scales(0)
+        nc.vector.tensor_copy(
+            out=wa_dealt_scales[:].rearrange("p (t m) -> p t m", t=PACK),
+            in_=wa_raw_scales[:].rearrange("p (m t) -> p t m", t=PACK),
+        )
+        gather_words(1)
+
+        old = [sb.tile([P, M], F32, name=f"old{b}", tag=f"early_late_{b}", align_bytes=64) for b in range(BLOCKS)]
+        for b in range(BLOCKS):
+            nc.sync.dma_start(out=old[b][:], in_=store[b * P : (b + 1) * P, :])
+
+        quarters = I // QUARTER
+        z = [psum.tile([P, PACK, QUARTER], F32, name=f"z{q}") for q in range(quarters)]
+        pieces = ((0, QUARTER), (QUARTER, QUARTER), (HALF, HALF))
+        w_tags = ("after_quantise1", "w1", "w2")
+        w = [sb.tile([P, n, PACK], BF16, name=f"w{s}", tag=w_tags[s], align_bytes=64) for s, (first, n) in enumerate(pieces)]
+        w_codes = [sb.tile([P, n], U32, name=f"w_codes{s}", align_bytes=64) for s, (first, n) in enumerate(pieces)]
+        w_scales = [sb.tile([P, n], U8, name=f"w_scales{s}", align_bytes=64) for s, (first, n) in enumerate(pieces)]
+        o = [sb.tile([P, I], F32, name=f"o{b}") for b in range(BLOCKS)]
+
+        def first_product(q):
+            h, within = divmod(q * QUARTER, HALF)
+            cols = slice(within, within + QUARTER)
+            for t in range(PACK):
+                nc.tensor.matmul_mx(
+                    z[q][:, t, :],
+                    lhsT=wa_dealt[:, t * P : (t + 1) * P].bitcast(FP8X4),
+                    lhsT_scale=wa_dealt_scales[:, t * P : (t + 1) * P],
+                    rhs=picked_words[h][:, cols].bitcast(FP4X4),
+                    rhs_scale=picked_scales[h][:, cols],
+                    start=True,
+                    stop=True,
+                )
+
+        def weigh(q):
+            s = min(q, 2)
+            within = q * QUARTER - pieces[s][0]
+            nc.vector.tensor_tensor(
+                w[s][:, within : within + QUARTER, :],
+                z[q][:].rearrange("p t n -> p n t"),
+                kf_sb[:].unsqueeze(1).to_broadcast([P, QUARTER, PACK]),
+                MULT,
+            )
+
+        def quantise(s):
+            nc.vector.quantize_mx(w_codes[s][:].bitcast(FP8X4), w_scales[s][:], w[s][:].rearrange("p n t -> p (n t)"))
+
+        def second_product(s, b, bank):
+            nc.tensor.matmul_mx(
+                bank,
+                lhsT=wo_sb[:, b * P : (b + 1) * P].bitcast(FP8X4),
+                lhsT_scale=wo_sb_scales[:, b * P : (b + 1) * P],
+                rhs=w_codes[s][:].bitcast(FP8X4),
+                rhs_scale=w_scales[s][:],
+                start=True,
+                stop=True,
+            )
+
+        def window(b, s):
+            return placed[b][:].indirect(entries(put_list, *pieces[s]))
+
+        def slots(b, s):
+            first, n = pieces[s]
+            return o[b][:, first : first + n]
+
+        def early_piece(s):
+            bank = psum.tile([P, BLOCKS, QUARTER], F32, name=f"o_early{s}")
+            for b in (1, 0):
+                second_product(s, b, bank[:, b, :])
+            for b in (1, 0):
+                nc.scalar.copy(slots(b, s), bank[:, b, :])
+            for b in (1, 0):
+                nc.scalar.activation(window(b, s), slots(b, s), COPY)
+
+        first_product(0)
+        first_product(1)
+        weigh(0)
+        quantise(0)
+        gather_scales(1)
+        early_piece(0)
+        first_product(2)
+        weigh(1)
+        first_product(3)
+        quantise(1)
+        early_piece(1)
+        weigh(2)
+        weigh(3)
+        quantise(2)
+        late = [psum.tile([P, HALF], F32, name=f"o_late{b}") for b in range(BLOCKS)]
+        for b in (1, 0):
+            second_product(2, b, late[b][:])
+        nc.vector.tensor_copy(slots(1, 2), late[1][:])
+        nc.vector.tensor_copy(window(1, 2), slots(1, 2))
+        nc.scalar.copy(slots(0, 2), late[0][:])
+        nc.scalar.activation(window(0, 2), slots(0, 2), COPY)
+
+        c1 = [sb.tile([P, M], F32, name=f"c1_{b}") for b in range(BLOCKS)]
+        for b in (1, 0):
+            nc.vector.tensor_tensor(c1[b][:], old[b][:], placed[b][:], ADD)
+
+        got1 = sb.tile([P, I], F32, name="got1")
+        nc.scalar.activation(got1[:], c1[1][:].indirect(get_list[:]), COPY)
+        got0 = sb.tile([P, HALF], F32, name="got0")
+        nc.scalar.activation(got0[:], c1[0][:].indirect(entries(get_list, HALF, HALF)), COPY)
+
+        y0a = sb.tile([P, HALF], F32, name="y0a")
+        nc.vector.tensor_tensor(y0a[:], c1[0][:].indirect(entries(get_list, 0, HALF)), o[0][:, :HALF], SUBTRACT)
+        nc.sync.dma_start(out=out[:P, :HALF], in_=y0a[:])
+        y1 = sb.tile([P, I], F32, name="y1")
+        nc.vector.tensor_tensor(y1[:], got1[:], o[1][:], SUBTRACT)
+        nc.sync.dma_start(out=out[P:, :], in_=y1[:])
+        y0b = sb.tile([P, HALF], F32, name="y0b")
+        nc.vector.tensor_tensor(y0b[:], got0[:], o[0][:, HALF:], SUBTRACT)
+        nc.sync.dma_start(out=out[:P, HALF:], in_=y0b[:])

@@ -86,8 +86,8 @@ def tile_attend_outputsback_kernel(
         nc.sync.dma_start(get_list[:], offs3)
 
         nc.scalar.copy(
-            out=wa_dealt[:].rearrange("p (t m) -> p t m", t=PACK),
-            in_=wa_raw[:].rearrange("p (m t) -> p t m", t=PACK),
+            out=wa_dealt[:].rearrange("p (t m) -> p m t", t=PACK),
+            in_=wa_raw[:].rearrange("p (m t) -> p m t", t=PACK),
         )
         picked_words = [sb.tile([P, HALF], U16, name=f"picked_words{h}", align_bytes=64) for h in range(2)]
         picked_scales = {}
@@ -119,7 +119,8 @@ def tile_attend_outputsback_kernel(
         w = [sb.tile([P, n, PACK], BF16, name=f"w{s}", tag=w_tags[s], align_bytes=64) for s, (first, n) in enumerate(pieces)]
         w_codes = [sb.tile([P, n], U32, name=f"w_codes{s}", align_bytes=64) for s, (first, n) in enumerate(pieces)]
         w_scales = [sb.tile([P, n], U8, name=f"w_scales{s}", align_bytes=64) for s, (first, n) in enumerate(pieces)]
-        o = [sb.tile([P, I], F32, name=f"o{b}") for b in range(BLOCKS)]
+        o_both = sb.tile([P, BLOCKS, I], F32, name="o_both")
+        o = [o_both[:, b, :] for b in range(BLOCKS)]
 
         def first_product(q):
             h, within = divmod(q * QUARTER, HALF)
@@ -139,9 +140,9 @@ def tile_attend_outputsback_kernel(
             s = min(q, 2)
             within = q * QUARTER - pieces[s][0]
             nc.vector.tensor_tensor(
-                w[s][:, within : within + QUARTER, :],
-                z[q][:].rearrange("p t n -> p n t"),
-                kf_sb[:].unsqueeze(1).to_broadcast([P, QUARTER, PACK]),
+                w[s][:, within : within + QUARTER, :].rearrange("p (c i) t -> p c t i", i=2),
+                z[q][:].rearrange("p t (c i) -> p c t i", i=2),
+                kf_sb[:].unsqueeze(1).unsqueeze(3).to_broadcast([P, QUARTER // 2, PACK, 2]),
                 MULT,
             )
 
@@ -170,8 +171,7 @@ def tile_attend_outputsback_kernel(
             bank = psum.tile([P, BLOCKS, QUARTER], F32, name=f"o_early{s}")
             for b in (1, 0):
                 second_product(s, b, bank[:, b, :])
-            for b in (1, 0):
-                nc.scalar.copy(slots(b, s), bank[:, b, :])
+            nc.scalar.copy(o_both[:, :, s * QUARTER : (s + 1) * QUARTER], bank[:])
             for b in (1, 0):
                 nc.scalar.activation(window(b, s), slots(b, s), COPY)
 
@@ -210,7 +210,7 @@ def tile_attend_outputsback_kernel(
         nc.vector.tensor_tensor(y0a[:], c1[0][:].indirect(entries(get_list, 0, HALF)), o[0][:, :HALF], SUBTRACT)
         nc.sync.dma_start(out=out[:P, :HALF], in_=y0a[:])
         y1 = sb.tile([P, I], F32, name="y1")
-        nc.vector.tensor_tensor(y1[:], got1[:], o[1][:], SUBTRACT)
+        nc.vector.tensor_tensor(y1[:], got1[:], o[1], SUBTRACT)
         nc.sync.dma_start(out=out[P:, :], in_=y1[:])
         y0b = sb.tile([P, HALF], F32, name="y0b")
         nc.vector.tensor_tensor(y0b[:], got0[:], o[0][:, HALF:], SUBTRACT)

@@ -30,14 +30,6 @@ def load_scale_rows(queue, plane, rows, q):
     queue.dma_start(out=plane[32 * q : 32 * q + 4, :].bitcast(I32), in_=rows[4 * q : 4 * q + 4, :].bitcast(I32))
 
 
-def load_scale_rows_repeated(queue, plane, rows, q):
-    words = rows[4 * q : 4 * q + 4, :].bitcast(I32)
-    queue.dma_start(
-        out=plane[32 * q : 32 * q + 32, :].bitcast(I32),
-        in_=words.unsqueeze(0).to_broadcast([8, 4, words.shape[1]]),
-    )
-
-
 def entries(offsets, first, count):
     return offsets[:, first // LIST_ROWS : (first + count) // LIST_ROWS]
 
@@ -53,69 +45,67 @@ def tile_attend_outputsback_kernel(
         page_list = sb.tile([P, I // LIST_ROWS], U16, name="page_list")
         put_list = sb.tile([P, I // LIST_ROWS], U16, name="put_list")
         get_list = sb.tile([P, I // LIST_ROWS], U16, name="get_list")
-        page_words = sb.tile([P, T], U16, name="page_words", tag="early_late_1", align_bytes=64)
+        page_words = sb.tile([P, T], U16, name="page_words", align_bytes=64)
         page_scales = sb.tile([P, T], U8, name="page_scales", align_bytes=64)
-        wa_raw = sb.tile([P, K], U32, name="wa_raw", tag="early_late_0", align_bytes=64)
-        wa_raw_scales = sb.tile([P, K], U8, name="wa_raw_scales", align_bytes=64)
+        wa_raw = sb.tile([P, K], U32, name="wa_raw", tag="weights", align_bytes=64)
+        wa_raw_scales = sb.tile([P, K], U8, name="wa_raw_scales", tag="scales1", align_bytes=64)
         wa_dealt = sb.tile([P, K], U32, name="wa_dealt", align_bytes=64)
         wa_dealt_scales = sb.tile([P, K], U8, name="wa_dealt_scales", align_bytes=64)
-        wo_sb = sb.tile([P, E], U32, name="wo_sb", align_bytes=64)
         wo_sb_scales = sb.tile([P, E], U8, name="wo_sb_scales", align_bytes=64)
         kf_sb = sb.tile([P, PACK], F32, name="kf_sb")
         placed = [sb.tile([P, M], F32, name=f"placed{b}") for b in range(BLOCKS)]
 
-        nc.vector.memset(wo_sb_scales[:].bitcast(I32), 0)
+        for plane in (page_scales, wa_raw_scales, wo_sb_scales):
+            nc.vector.memset(plane[:].bitcast(I32), 0)
         for b in range(BLOCKS):
             nc.vector.memset(placed[b][:], 0.0)
 
+        nc.gpsimd.dma_start(out=wa_raw[:].bitcast(I32), in_=wa_words[0].rearrange("p n t -> p (n t)").bitcast(I32))
         nc.sync.dma_start(page_list[:], offs)
-        for q in range(2):
-            load_scale_rows_repeated(nc.sync, page_scales, pages_scales[0], q)
         nc.sync.dma_start(out=page_words[:].bitcast(I32), in_=pages_words[0].bitcast(I32))
-        for q in range(2, 4):
-            load_scale_rows_repeated(nc.sync, page_scales, pages_scales[0], q)
-        load_scale_rows_repeated(nc.sync, wa_raw_scales, wa_scales[0], 0)
-        nc.sync.dma_start(out=wa_raw[:].bitcast(I32), in_=wa_words[0].rearrange("p n t -> p (n t)").bitcast(I32))
-        for q in range(1, 4):
-            load_scale_rows_repeated(nc.sync, wa_raw_scales, wa_scales[0], q)
-        nc.gpsimd.dma_start(out=kf_sb[:], in_=kf.rearrange("(p t) one -> p (t one)", t=PACK))
-        nc.gpsimd.dma_start(out=wo_sb[:].bitcast(I32), in_=wo_words[0].rearrange("p n t -> p (n t)").bitcast(I32))
-        for q in range(4):
-            load_scale_rows(nc.sync, wo_sb_scales, wo_scales[0], q)
         nc.sync.dma_start(put_list[:], offs2)
         nc.sync.dma_start(get_list[:], offs3)
+        nc.sync.dma_start(out=kf_sb[:], in_=kf.rearrange("(p t) one -> p (t one)", t=PACK))
+        for q in range(4):
+            load_scale_rows(nc.sync, page_scales, pages_scales[0], q)
+        for q in range(4):
+            load_scale_rows(nc.sync, wa_raw_scales, wa_scales[0], q)
+        for q in range(4):
+            load_scale_rows(nc.sync, wo_sb_scales, wo_scales[0], q)
 
         nc.scalar.copy(
             out=wa_dealt[:].rearrange("p (t m) -> p m t", t=PACK),
             in_=wa_raw[:].rearrange("p (m t) -> p m t", t=PACK),
         )
-        picked_words = [sb.tile([P, HALF], U16, name=f"picked_words{h}", align_bytes=64) for h in range(2)]
+        wo_sb = sb.tile([P, E], U32, name="wo_sb", tag="weights", align_bytes=64)
+        nc.sync.dma_start(out=wo_sb[:].bitcast(I32), in_=wo_words[0].rearrange("p n t -> p (n t)").bitcast(I32))
+        word_tags = ("early_late_1", "early_late_0")
+        picked_words = [sb.tile([P, HALF], U16, name=f"picked_words{h}", tag=word_tags[h], align_bytes=64) for h in range(2)]
         picked_scales = {}
 
         def gather_words(h):
             nc.vector.tensor_copy(picked_words[h][:], page_words[:].indirect(entries(page_list, h * HALF, HALF)))
 
         def gather_scales(h):
-            picked = sb.tile([P, HALF], U8, name=f"picked_scales{h}", tag=f"after_quantise{h}", align_bytes=64)
+            picked = sb.tile([P, HALF], U8, name=f"picked_scales{h}", tag=f"scales{h}", align_bytes=64)
             nc.vector.tensor_copy(picked[:], page_scales[:].indirect(entries(page_list, h * HALF, HALF)))
             picked_scales.setdefault(h, picked)
 
         gather_words(0)
         gather_scales(0)
-        nc.vector.tensor_copy(
-            out=wa_dealt_scales[:].rearrange("p (t m) -> p t m", t=PACK),
-            in_=wa_raw_scales[:].rearrange("p (m t) -> p t m", t=PACK),
-        )
+        for places in (slice(0, 2), slice(2, 4)):
+            nc.vector.tensor_copy(
+                out=wa_dealt_scales[:].rearrange("p (t m) -> p t m", t=PACK)[:, places, :],
+                in_=wa_raw_scales[:].rearrange("p (m t) -> p t m", t=PACK)[:, places, :],
+            )
         gather_words(1)
-
-        old = [sb.tile([P, M], F32, name=f"old{b}", tag=f"early_late_{b}", align_bytes=64) for b in range(BLOCKS)]
-        for b in range(BLOCKS):
-            nc.sync.dma_start(out=old[b][:], in_=store[b * P : (b + 1) * P, :])
+        gather_scales(1)
 
         quarters = I // QUARTER
-        z = [psum.tile([P, PACK, QUARTER], F32, name=f"z{q}") for q in range(quarters)]
+        z = {}
+        z_banks = ("bank0", "bank1", "bank0", "bank2")
         pieces = ((0, QUARTER), (QUARTER, QUARTER), (HALF, HALF))
-        w_tags = ("after_quantise1", "w1", "w2")
+        w_tags = ("w0", "w1", "w2")
         w = [sb.tile([P, n, PACK], BF16, name=f"w{s}", tag=w_tags[s], align_bytes=64) for s, (first, n) in enumerate(pieces)]
         w_codes = [sb.tile([P, n], U32, name=f"w_codes{s}", align_bytes=64) for s, (first, n) in enumerate(pieces)]
         w_scales = [sb.tile([P, n], U8, name=f"w_scales{s}", align_bytes=64) for s, (first, n) in enumerate(pieces)]
@@ -125,6 +115,7 @@ def tile_attend_outputsback_kernel(
         def first_product(q):
             h, within = divmod(q * QUARTER, HALF)
             cols = slice(within, within + QUARTER)
+            z.setdefault(q, psum.tile([P, PACK, QUARTER], F32, name=f"z{q}", tag=z_banks[q]))
             for t in range(PACK):
                 nc.tensor.matmul_mx(
                     z[q][:, t, :],
@@ -135,6 +126,12 @@ def tile_attend_outputsback_kernel(
                     start=True,
                     stop=True,
                 )
+
+        old = {}
+
+        def load_old(b):
+            old.setdefault(b, sb.tile([P, M], F32, name=f"old{b}", tag=f"early_late_{b}", align_bytes=64))
+            nc.sync.dma_start(out=old[b][:], in_=store[b * P : (b + 1) * P, :])
 
         def weigh(q):
             s = min(q, 2)
@@ -167,26 +164,28 @@ def tile_attend_outputsback_kernel(
             first, n = pieces[s]
             return o[b][:, first : first + n]
 
-        def early_piece(s):
-            bank = psum.tile([P, BLOCKS, QUARTER], F32, name=f"o_early{s}")
+        def early_piece(s, on_scalar):
+            bank = psum.tile([P, BLOCKS, QUARTER], F32, name=f"o_early{s}", tag=f"bank{2 + s}")
             for b in (1, 0):
                 second_product(s, b, bank[:, b, :])
             nc.scalar.copy(o_both[:, :, s * QUARTER : (s + 1) * QUARTER], bank[:])
-            for b in (1, 0):
+            for b in on_scalar:
                 nc.scalar.activation(window(b, s), slots(b, s), COPY)
 
         first_product(0)
         first_product(1)
+        load_old(1)
         weigh(0)
         quantise(0)
-        gather_scales(1)
-        early_piece(0)
+        early_piece(0, (0,))
         first_product(2)
         weigh(1)
         first_product(3)
+        load_old(0)
         quantise(1)
-        early_piece(1)
         weigh(2)
+        nc.vector.tensor_copy(window(1, 0), slots(1, 0))
+        early_piece(1, (1, 0))
         weigh(3)
         quantise(2)
         late = [psum.tile([P, HALF], F32, name=f"o_late{b}") for b in range(BLOCKS)]

from contextlib import ExitStack

import concourse.mybir as mybir

D, K, T, M, I, E = 512, 512, 2048, 1024, 512, 256
FLOPS = 2 * D * K * I + 2 * K * E * I

F32 = mybir.dt.float32
BF16 = mybir.dt.bfloat16
I32 = mybir.dt.int32
U32 = mybir.dt.uint32
U16 = mybir.dt.uint16
U8 = mybir.dt.uint8
FP8X4 = mybir.dt.float8_e4m3fn_x4
FP4X4 = mybir.dt.float4_e2m1fn_x4
MULT = mybir.AluOpType.mult
ADD = mybir.AluOpType.add
SUBTRACT = mybir.AluOpType.subtract
COPY = mybir.ActivationFunctionType.Copy

P = 128
PACK = 4
LIST_ROWS = 16
HALF = 256
QUARTER = 128
BLOCKS = E // P


def load_scale_rows(queue, plane, rows, q):
    queue.dma_start(out=plane[32 * q : 32 * q + 4, :].bitcast(I32), in_=rows[4 * q : 4 * q + 4, :].bitcast(I32))


def entries(offsets, first, count):
    return offsets[:, first // LIST_ROWS : (first + count) // LIST_ROWS]


def tile_attend_outputsback_kernel(
    tc, pages_words, pages_scales, wa_words, wa_scales, kf, wo_words, wo_scales, store, offs, offs2, offs3, out
):
    nc = tc.nc
    with ExitStack() as ctx:
        sb = ctx.enter_context(tc.tile_pool(name="sb", bufs=1))
        psum = ctx.enter_context(tc.psum_pool(name="psum", bufs=1))

        page_list = sb.tile([P, I // LIST_ROWS], U16, name="page_list")
        put_list = sb.tile([P, I // LIST_ROWS], U16, name="put_list")
        get_list = sb.tile([P, I // LIST_ROWS], U16, name="get_list")
        page_words = sb.tile([P, T], U16, name="page_words", align_bytes=64)
        page_scales = sb.tile([P, T], U8, name="page_scales", align_bytes=64)
        wa_raw = sb.tile([P, K], U32, name="wa_raw", tag="weights", align_bytes=64)
        wa_raw_scales = sb.tile([P, K], U8, name="wa_raw_scales", tag="scales1", align_bytes=64)
        wa_dealt = sb.tile([P, K], U32, name="wa_dealt", align_bytes=64)
        wa_dealt_scales = sb.tile([P, K], U8, name="wa_dealt_scales", align_bytes=64)
        wo_sb_scales = sb.tile([P, E], U8, name="wo_sb_scales", align_bytes=64)
        kf_sb = sb.tile([P, PACK], F32, name="kf_sb")
        placed = [sb.tile([P, M], F32, name=f"placed{b}") for b in range(BLOCKS)]

        for plane in (page_scales, wa_raw_scales, wo_sb_scales):
            nc.vector.memset(plane[:].bitcast(I32), 0)
        for b in range(BLOCKS):
            nc.vector.memset(placed[b][:], 0.0)

        nc.gpsimd.dma_start(out=wa_raw[:].bitcast(I32), in_=wa_words[0].rearrange("p n t -> p (n t)").bitcast(I32))
        nc.sync.dma_start(page_list[:], offs)
        nc.sync.dma_start(out=page_words[:].bitcast(I32), in_=pages_words[0].bitcast(I32))
        nc.sync.dma_start(put_list[:], offs2)
        nc.sync.dma_start(get_list[:], offs3)
        nc.sync.dma_start(out=kf_sb[:], in_=kf.rearrange("(p t) one -> p (t one)", t=PACK))
        for q in range(4):
            load_scale_rows(nc.sync, page_scales, pages_scales[0], q)
        for q in range(4):
            load_scale_rows(nc.sync, wa_raw_scales, wa_scales[0], q)
        for q in range(4):
            load_scale_rows(nc.sync, wo_sb_scales, wo_scales[0], q)

        nc.scalar.copy(
            out=wa_dealt[:].rearrange("p (t m) -> p m t", t=PACK),
            in_=wa_raw[:].rearrange("p (m t) -> p m t", t=PACK),
        )
        wo_sb = sb.tile([P, E], U32, name="wo_sb", tag="weights", align_bytes=64)
        nc.sync.dma_start(out=wo_sb[:].bitcast(I32), in_=wo_words[0].rearrange("p n t -> p (n t)").bitcast(I32))
        word_tags = ("early_late_1", "early_late_0")
        picked_words = [sb.tile([P, HALF], U16, name=f"picked_words{h}", tag=word_tags[h], align_bytes=64) for h in range(2)]
        picked_scales = {}

        def gather_words(h):
            nc.vector.tensor_copy(picked_words[h][:], page_words[:].indirect(entries(page_list, h * HALF, HALF)))

        def gather_scales(h):
            picked = sb.tile([P, HALF], U8, name=f"picked_scales{h}", tag=f"scales{h}", align_bytes=64)
            nc.vector.tensor_copy(picked[:], page_scales[:].indirect(entries(page_list, h * HALF, HALF)))
            picked_scales.setdefault(h, picked)

        gather_words(0)
        gather_scales(0)
        for places in (slice(0, 2), slice(2, 4)):
            nc.vector.tensor_copy(
                out=wa_dealt_scales[:].rearrange("p (t m) -> p t m", t=PACK)[:, places, :],
                in_=wa_raw_scales[:].rearrange("p (m t) -> p t m", t=PACK)[:, places, :],
            )
        gather_words(1)
        gather_scales(1)

        quarters = I // QUARTER
        z = {}
        z_banks = ("bank0", "bank1", "bank0", "bank2")
        pieces = ((0, QUARTER), (QUARTER, QUARTER), (HALF, HALF))
        w_tags = ("w0", "w1", "w2")
        w = [sb.tile([P, n, PACK], BF16, name=f"w{s}", tag=w_tags[s], align_bytes=64) for s, (first, n) in enumerate(pieces)]
        w_codes = [sb.tile([P, n], U32, name=f"w_codes{s}", align_bytes=64) for s, (first, n) in enumerate(pieces)]
        w_scales = [sb.tile([P, n], U8, name=f"w_scales{s}", align_bytes=64) for s, (first, n) in enumerate(pieces)]
        o_both = sb.tile([P, BLOCKS, I], F32, name="o_both")
        o = [o_both[:, b, :] for b in range(BLOCKS)]

        def first_product(q):
            h, within = divmod(q * QUARTER, HALF)
            cols = slice(within, within + QUARTER)
            z.setdefault(q, psum.tile([P, PACK, QUARTER], F32, name=f"z{q}", tag=z_banks[q]))
            for t in range(PACK):
                nc.tensor.matmul_mx(
                    z[q][:, t, :],
                    lhsT=wa_dealt[:, t * P : (t + 1) * P].bitcast(FP8X4),
                    lhsT_scale=wa_dealt_scales[:, t * P : (t + 1) * P],
                    rhs=picked_words[h][:, cols].bitcast(FP4X4),
                    rhs_scale=picked_scales[h][:, cols],
                    start=True,
                    stop=True,
                )

        old = {}

        def load_old(b):
            old.setdefault(b, sb.tile([P, M], F32, name=f"old{b}", tag=f"early_late_{b}", align_bytes=64))
            nc.sync.dma_start(out=old[b][:], in_=store[b * P : (b + 1) * P, :])

        def weigh(q):
            s = min(q, 2)
            within = q * QUARTER - pieces[s][0]
            nc.vector.tensor_tensor(
                w[s][:, within : within + QUARTER, :].rearrange("p (c i) t -> p c t i", i=2),
                z[q][:].rearrange("p t (c i) -> p c t i", i=2),
                kf_sb[:].unsqueeze(1).unsqueeze(3).to_broadcast([P, QUARTER // 2, PACK, 2]),
                MULT,
            )

        def quantise(s):
            nc.vector.quantize_mx(w_codes[s][:].bitcast(FP8X4), w_scales[s][:], w[s][:].rearrange("p n t -> p (n t)"))

        def second_product(s, b, bank):
            nc.tensor.matmul_mx(
                bank,
                lhsT=wo_sb[:, b * P : (b + 1) * P].bitcast(FP8X4),
                lhsT_scale=wo_sb_scales[:, b * P : (b + 1) * P],
                rhs=w_codes[s][:].bitcast(FP8X4),
                rhs_scale=w_scales[s][:],
                start=True,
                stop=True,
            )

        def window(b, s):
            return placed[b][:].indirect(entries(put_list, *pieces[s]))

        def slots(b, s):
            first, n = pieces[s]
            return o[b][:, first : first + n]

        def early_piece(s, on_scalar):
            bank = psum.tile([P, BLOCKS, QUARTER], F32, name=f"o_early{s}", tag=f"bank{2 + s}")
            for b in (1, 0):
                second_product(s, b, bank[:, b, :])
            nc.scalar.copy(o_both[:, :, s * QUARTER : (s + 1) * QUARTER], bank[:])
            for b in on_scalar:
                nc.scalar.activation(window(b, s), slots(b, s), COPY)

        first_product(0)
        first_product(1)
        load_old(1)
        weigh(0)
        quantise(0)
        early_piece(0, (0,))
        first_product(2)
        weigh(1)
        first_product(3)
        load_old(0)
        quantise(1)
        weigh(2)
        nc.vector.tensor_copy(window(1, 0), slots(1, 0))
        early_piece(1, (1, 0))
        weigh(3)
        quantise(2)
        late = [psum.tile([P, HALF], F32, name=f"o_late{b}") for b in range(BLOCKS)]
        for b in (1, 0):
            second_product(2, b, late[b][:])
        nc.vector.tensor_copy(slots(1, 2), late[1][:])
        nc.vector.tensor_copy(window(1, 2), slots(1, 2))
        nc.scalar.copy(slots(0, 2), late[0][:])
        nc.scalar.activation(window(0, 2), slots(0, 2), COPY)

        c1 = [sb.tile([P, M], F32, name=f"c1_{b}") for b in range(BLOCKS)]
        for b in (1, 0):
            nc.vector.tensor_tensor(c1[b][:], old[b][:], placed[b][:], ADD)

        got1 = sb.tile([P, I], F32, name="got1")
        nc.scalar.activation(got1[:], c1[1][:].indirect(get_list[:]), COPY)
        got0 = sb.tile([P, HALF], F32, name="got0")
        nc.scalar.activation(got0[:], c1[0][:].indirect(entries(get_list, HALF, HALF)), COPY)

        y0a = sb.tile([P, HALF], F32, name="y0a")
        nc.vector.tensor_tensor(y0a[:], c1[0][:].indirect(entries(get_list, 0, HALF)), o[0][:, :HALF], SUBTRACT)
        nc.sync.dma_start(out=out[:P, :HALF], in_=y0a[:])
        y1 = sb.tile([P, I], F32, name="y1")
        nc.vector.tensor_tensor(y1[:], got1[:], o[1], SUBTRACT)
        nc.sync.dma_start(out=out[P:, :], in_=y1[:])
        y0b = sb.tile([P, HALF], F32, name="y0b")
        nc.vector.tensor_tensor(y0b[:], got0[:], o[0][:, HALF:], SUBTRACT)
        nc.sync.dma_start(out=out[:P, HALF:], in_=y0b[:])
